import numpy as np
import ml_dtypes

BF16 = ml_dtypes.bfloat16


def bf(x):
    return np.asarray(x, np.float32).astype(BF16)


def f32(x):
    return np.asarray(x, np.float32)


def f64(x):
    return np.asarray(x).astype(np.float64)


def striped(idx):
    return np.tile(idx.reshape(-1, 16).T, (8, 1))


def rows(idx, k):
    return np.tile(idx, (k, 1))


def look(tab, idx):
    return np.take_along_axis(f64(tab), rows(idx, len(tab)), axis=1)


K, S, V, N = 256, 2048, 2048, 2048


def setup_inputs():
    return {"tab": f32(np.random.standard_normal((2, K, S))), "y": f32(np.random.standard_normal((K, V))), "offs": striped(np.random.permutation(S)[:N])}


def reference(tab, y, offs):
    idx = offs[:16].T.reshape(-1)
    x = (look(tab[0], idx) + f64(y)) * (np.tanh(look(tab[1], idx)))
    return x

@@ -1,0 +1,42 @@
+import concourse.mybir as mybir
+
+F32, U16 = mybir.dt.float32, mybir.dt.uint16
+ADD, MULT = mybir.AluOpType.add, mybir.AluOpType.mult
+TANH = mybir.ActivationFunctionType.Tanh
+
+P = 128
+GROUP = 16
+PIECE = 512
+
+
+def tile_lookup_vg_addtanh_out_kernel(tc, tab, y, offs, out):
+    nc = tc.nc
+    rows, places = tab.shape[1], tab.shape[2]
+    entries = y.shape[1]
+    blocks, pieces = rows // P, entries // PIECE
+
+    with tc.tile_pool(name="sbuf", bufs=1) as sbuf:
+        offsets = sbuf.tile([P, entries // GROUP], U16, name="offsets")
+        values = [sbuf.tile([P, places], F32, name=f"values{b}") for b in range(blocks)]
+        gates = [sbuf.tile([P, places], F32, name=f"gates{b}") for b in range(blocks)]
+        stream = [sbuf.tile([P, entries], F32, name=f"stream{b}") for b in range(blocks)]
+        summed = [sbuf.tile([P, entries], F32, name=f"summed{b}") for b in range(blocks)]
+        opened = [sbuf.tile([P, entries], F32, name=f"opened{b}") for b in range(blocks)]
+        product = [sbuf.tile([P, entries], F32, name=f"product{b}") for b in range(blocks)]
+
+        nc.sync.dma_start(offsets[:], offs)
+        for b in range(blocks):
+            block_rows = slice(b * P, (b + 1) * P)
+            nc.sync.dma_start(values[b][:], tab[0, block_rows, :])
+            nc.sync.dma_start(gates[b][:], tab[1, block_rows, :])
+            nc.sync.dma_start(stream[b][:], y[block_rows, :])
+
+        for b in range(blocks):
+            block_rows = slice(b * P, (b + 1) * P)
+            for k in range(pieces):
+                cols = slice(k * PIECE, (k + 1) * PIECE)
+                listed = offsets[:, k * PIECE // GROUP : (k + 1) * PIECE // GROUP]
+                nc.vector.tensor_tensor(summed[b][:, cols], values[b][:].indirect(listed), stream[b][:, cols], ADD)
+                nc.scalar.activation(opened[b][:, cols], gates[b][:].indirect(listed), TANH)
+                nc.vector.tensor_tensor(product[b][:, cols], summed[b][:, cols], opened[b][:, cols], MULT)
+                nc.sync.dma_start(out[block_rows, cols], product[b][:, cols])

@@ -7,6 +7,7 @@ TANH = mybir.ActivationFunctionType.Tanh
 P = 128
 GROUP = 16
 PIECE = 512
+LAG = 2
 
 
 def tile_lookup_vg_addtanh_out_kernel(tc, tab, y, offs, out):
@@ -15,28 +16,48 @@ def tile_lookup_vg_addtanh_out_kernel(tc, tab, y, offs, out):
     entries = y.shape[1]
     blocks, pieces = rows // P, entries // PIECE
 
-    with tc.tile_pool(name="sbuf", bufs=1) as sbuf:
+    with tc.tile_pool(name="sbuf", bufs=1) as sbuf, tc.tile_pool(name="ring", bufs=LAG + 1) as ring:
         offsets = sbuf.tile([P, entries // GROUP], U16, name="offsets")
         values = [sbuf.tile([P, places], F32, name=f"values{b}") for b in range(blocks)]
         gates = [sbuf.tile([P, places], F32, name=f"gates{b}") for b in range(blocks)]
         stream = [sbuf.tile([P, entries], F32, name=f"stream{b}") for b in range(blocks)]
-        summed = [sbuf.tile([P, entries], F32, name=f"summed{b}") for b in range(blocks)]
         opened = [sbuf.tile([P, entries], F32, name=f"opened{b}") for b in range(blocks)]
         product = [sbuf.tile([P, entries], F32, name=f"product{b}") for b in range(blocks)]
 
+        def block_rows(b):
+            return slice(b * P, (b + 1) * P)
+
+        def piece_cols(k):
+            return slice(k * PIECE, (k + 1) * PIECE)
+
+        def piece_offsets(k):
+            return offsets[:, k * PIECE // GROUP : (k + 1) * PIECE // GROUP]
+
         nc.sync.dma_start(offsets[:], offs)
         for b in range(blocks):
-            block_rows = slice(b * P, (b + 1) * P)
-            nc.sync.dma_start(values[b][:], tab[0, block_rows, :])
-            nc.sync.dma_start(gates[b][:], tab[1, block_rows, :])
-            nc.sync.dma_start(stream[b][:], y[block_rows, :])
-
-        for b in range(blocks):
-            block_rows = slice(b * P, (b + 1) * P)
+            nc.sync.dma_start(values[b][:], tab[0, block_rows(b), :])
             for k in range(pieces):
-                cols = slice(k * PIECE, (k + 1) * PIECE)
-                listed = offsets[:, k * PIECE // GROUP : (k + 1) * PIECE // GROUP]
-                nc.vector.tensor_tensor(summed[b][:, cols], values[b][:].indirect(listed), stream[b][:, cols], ADD)
-                nc.scalar.activation(opened[b][:, cols], gates[b][:].indirect(listed), TANH)
-                nc.vector.tensor_tensor(product[b][:, cols], summed[b][:, cols], opened[b][:, cols], MULT)
-                nc.sync.dma_start(out[block_rows, cols], product[b][:, cols])
+                if k == LAG:
+                    nc.sync.dma_start(gates[b][:], tab[1, block_rows(b), :])
+                nc.sync.dma_start(stream[b][:, piece_cols(k)], y[block_rows(b), piece_cols(k)])
+
+        zeros = sbuf.tile([P, 1], F32, name="zeros")
+        warm = sbuf.tile([P, 1], F32, name="warm")
+        nc.vector.memset(zeros[:], 0.0)
+        nc.scalar.activation(warm[:], zeros[:], TANH)
+
+        summed = {}
+        steps = [(b, k) for b in range(blocks) for k in range(pieces)]
+        for step in range(len(steps) + LAG):
+            if step < len(steps):
+                b, k = steps[step]
+                cols = piece_cols(k)
+                picked = values[b][:].indirect(piece_offsets(k))
+                summed[b, k] = ring.tile([P, PIECE], F32, name="summed")
+                nc.vector.tensor_tensor(summed[b, k][:], picked, stream[b][:, cols], ADD)
+            if step >= LAG:
+                b, k = steps[step - LAG]
+                cols = piece_cols(k)
+                nc.scalar.activation(opened[b][:, cols], gates[b][:].indirect(piece_offsets(k)), TANH)
+                nc.vector.tensor_tensor(product[b][:, cols], summed[b, k][:], opened[b][:, cols], MULT)
+                nc.sync.dma_start(out[block_rows(b), cols], product[b][:, cols])

@@ -15,49 +15,43 @@ def tile_lookup_vg_addtanh_out_kernel(tc, tab, y, offs, out):
     rows, places = tab.shape[1], tab.shape[2]
     entries = y.shape[1]
     blocks, pieces = rows // P, entries // PIECE
+    steps = [(b, k) for b in range(blocks) for k in range(pieces)]
 
-    with tc.tile_pool(name="sbuf", bufs=1) as sbuf, tc.tile_pool(name="ring", bufs=LAG + 1) as ring:
+    def block_rows(b):
+        return slice(b * P, (b + 1) * P)
+
+    def piece_cols(k):
+        return slice(k * PIECE, (k + 1) * PIECE)
+
+    with tc.tile_pool(name="sbuf", bufs=1) as sbuf:
         offsets = sbuf.tile([P, entries // GROUP], U16, name="offsets")
         values = [sbuf.tile([P, places], F32, name=f"values{b}") for b in range(blocks)]
         gates = [sbuf.tile([P, places], F32, name=f"gates{b}") for b in range(blocks)]
-        stream = [sbuf.tile([P, entries], F32, name=f"stream{b}") for b in range(blocks)]
-        opened = [sbuf.tile([P, entries], F32, name=f"opened{b}") for b in range(blocks)]
-        product = [sbuf.tile([P, entries], F32, name=f"product{b}") for b in range(blocks)]
-
-        def block_rows(b):
-            return slice(b * P, (b + 1) * P)
-
-        def piece_cols(k):
-            return slice(k * PIECE, (k + 1) * PIECE)
+        summed = [sbuf.tile([P, PIECE], F32, name=f"summed{s}") for s in range(len(steps))]
+        opened = [sbuf.tile([P, PIECE], F32, name=f"opened{s}") for s in range(len(steps))]
+        stream = [sbuf.tile([P, PIECE], F32, name=f"stream{s}") for s in range(len(steps) + LAG)]
 
         def piece_offsets(k):
             return offsets[:, k * PIECE // GROUP : (k + 1) * PIECE // GROUP]
 
         nc.sync.dma_start(offsets[:], offs)
-        for b in range(blocks):
-            nc.sync.dma_start(values[b][:], tab[0, block_rows(b), :])
-            for k in range(pieces):
-                if k == LAG:
-                    nc.sync.dma_start(gates[b][:], tab[1, block_rows(b), :])
-                nc.sync.dma_start(stream[b][:, piece_cols(k)], y[block_rows(b), piece_cols(k)])
+        for s, (b, k) in enumerate(steps):
+            if k == 0:
+                nc.sync.dma_start(values[b][:], tab[0, block_rows(b), :])
+            if k == LAG:
+                nc.sync.dma_start(gates[b][:], tab[1, block_rows(b), :])
+            nc.sync.dma_start(stream[s][:], y[block_rows(b), piece_cols(k)])
 
         zeros = sbuf.tile([P, 1], F32, name="zeros")
         warm = sbuf.tile([P, 1], F32, name="warm")
         nc.vector.memset(zeros[:], 0.0)
         nc.scalar.activation(warm[:], zeros[:], TANH)
 
-        summed = {}
-        steps = [(b, k) for b in range(blocks) for k in range(pieces)]
-        for step in range(len(steps) + LAG):
-            if step < len(steps):
-                b, k = steps[step]
-                cols = piece_cols(k)
-                picked = values[b][:].indirect(piece_offsets(k))
-                summed[b, k] = ring.tile([P, PIECE], F32, name="summed")
-                nc.vector.tensor_tensor(summed[b, k][:], picked, stream[b][:, cols], ADD)
-            if step >= LAG:
-                b, k = steps[step - LAG]
-                cols = piece_cols(k)
-                nc.scalar.activation(opened[b][:, cols], gates[b][:].indirect(piece_offsets(k)), TANH)
-                nc.vector.tensor_tensor(product[b][:, cols], summed[b, k][:], opened[b][:, cols], MULT)
-                nc.sync.dma_start(out[block_rows(b), cols], product[b][:, cols])
+        for s, (b, k) in enumerate(steps):
+            nc.scalar.activation(opened[s][:], gates[b][:].indirect(piece_offsets(k)), TANH)
+            nc.vector.tensor_tensor(summed[s][:], values[b][:].indirect(piece_offsets(k)), stream[s][:], ADD)
+
+        for s, (b, k) in enumerate(steps):
+            product = stream[s + LAG]
+            nc.vector.tensor_tensor(product[:], summed[s][:], opened[s][:], MULT)
+            nc.sync.dma_start(out[block_rows(b), piece_cols(k)], product[:])

import concourse.mybir as mybir

F32, U16 = mybir.dt.float32, mybir.dt.uint16
ADD, MULT = mybir.AluOpType.add, mybir.AluOpType.mult
TANH = mybir.ActivationFunctionType.Tanh

P = 128
GROUP = 16
PIECE = 512
LAG = 2


def tile_lookup_vg_addtanh_out_kernel(tc, tab, y, offs, out):
    nc = tc.nc
    rows, places = tab.shape[1], tab.shape[2]
    entries = y.shape[1]
    blocks, pieces = rows // P, entries // PIECE
    steps = [(b, k) for b in range(blocks) for k in range(pieces)]

    def block_rows(b):
        return slice(b * P, (b + 1) * P)

    def piece_cols(k):
        return slice(k * PIECE, (k + 1) * PIECE)

    with tc.tile_pool(name="sbuf", bufs=1) as sbuf:
        offsets = sbuf.tile([P, entries // GROUP], U16, name="offsets")
        values = [sbuf.tile([P, places], F32, name=f"values{b}") for b in range(blocks)]
        gates = [sbuf.tile([P, places], F32, name=f"gates{b}") for b in range(blocks)]
        summed = [sbuf.tile([P, PIECE], F32, name=f"summed{s}") for s in range(len(steps))]
        opened = [sbuf.tile([P, PIECE], F32, name=f"opened{s}") for s in range(len(steps))]
        stream = [sbuf.tile([P, PIECE], F32, name=f"stream{s}") for s in range(len(steps) + LAG)]

        def piece_offsets(k):
            return offsets[:, k * PIECE // GROUP : (k + 1) * PIECE // GROUP]

        nc.sync.dma_start(offsets[:], offs)
        for s, (b, k) in enumerate(steps):
            if k == 0:
                nc.sync.dma_start(values[b][:], tab[0, block_rows(b), :])
            if k == LAG:
                nc.sync.dma_start(gates[b][:], tab[1, block_rows(b), :])
            nc.sync.dma_start(stream[s][:], y[block_rows(b), piece_cols(k)])

        zeros = sbuf.tile([P, 1], F32, name="zeros")
        warm = sbuf.tile([P, 1], F32, name="warm")
        nc.vector.memset(zeros[:], 0.0)
        nc.scalar.activation(warm[:], zeros[:], TANH)

        for s, (b, k) in enumerate(steps):
            nc.scalar.activation(opened[s][:], gates[b][:].indirect(piece_offsets(k)), TANH)
            nc.vector.tensor_tensor(summed[s][:], values[b][:].indirect(piece_offsets(k)), stream[s][:], ADD)

        for s, (b, k) in enumerate(steps):
            product = stream[s + LAG]
            nc.vector.tensor_tensor(product[:], summed[s][:], opened[s][:], MULT)
            nc.sync.dma_start(out[block_rows(b), piece_cols(k)], product[:])
